import numpy as np
import ml_dtypes


def mxq(x, axis, fmt="e4m3"):
    dtype, down = {"e4m3": (ml_dtypes.float8_e4m3fn, 7), "e5m2": (ml_dtypes.float8_e5m2, 14)}[fmt]
    v = np.moveaxis(np.asarray(x, np.float32).astype(ml_dtypes.bfloat16).astype(np.float64), axis, -1)
    blocks = v.reshape(v.shape[:-1] + (-1, 32))
    amax = np.abs(blocks).max(-1, keepdims=True)
    byte = np.maximum(np.where(amax > 0, np.frexp(amax)[1] - 1 + 127, 0) - down, 1)
    scale = np.exp2(byte - 127.0)
    codes = (blocks / scale).astype(np.float32).astype(dtype).astype(np.float64)
    return np.moveaxis((codes * scale).reshape(v.shape), -1, axis)


WIDE = False


def mx_kscale(k):
    if not WIDE:
        return np.ones(k)
    levels = np.array([10, -10, 5, -5, 0])
    if k % 512:
        return np.exp2(np.random.permutation(np.resize(levels, k // 32))).repeat(32)
    a = np.empty((k // 512, 16))
    for p in range(k // 512):
        a[p, :8] = np.random.permutation(np.resize(levels, 8))
        for g in range(8):
            far = levels[np.abs(levels - a[p, g]) >= 10]
            a[p, g + 8] = far[np.random.randint(len(far))]
    return np.exp2(a.ravel()).repeat(32)


def f64(x):
    return np.asarray(x).astype(np.float64)


def striped(idx):
    return np.tile(idx.reshape(-1, 16).T, (8, 1)).astype(np.uint16)


def unstriped(offs):
    return offs[:16].T.reshape(-1).astype(np.int64)


def pack_weight(w):
    k, n = w.shape
    w = f64(np.asarray(w, np.float32).astype(ml_dtypes.bfloat16)).reshape(k // 32, 32, n)
    amax = np.abs(w).max(1)
    byte = np.clip(np.where(amax > 0, np.frexp(amax)[1] - 1 + 127 - 7, 1), 1, 254)
    scaled = (w * np.exp2(127.0 - byte)[:, None, :]).reshape(k, n).astype(np.float32)
    words = np.ascontiguousarray(scaled.reshape(k // 512, 128, 4, n).transpose(0, 1, 3, 2)).astype(ml_dtypes.float8_e4m3fn).view(np.uint8)
    return words, np.ascontiguousarray(byte.astype(np.uint8).reshape(k // 512, 16, n))


def unpack_weight(words, scales):
    g, p, n, _ = words.shape
    vals = np.ascontiguousarray(words).view(ml_dtypes.float8_e4m3fn).astype(np.float64) * np.repeat(np.exp2(scales.astype(np.float64) - 127.0), 8, axis=1)[..., None]
    return vals.transpose(0, 1, 3, 2).reshape(g * 512, n)


def gelu(v):
    return 0.5 * v * (1.0 + np.tanh(np.sqrt(2.0 / np.pi) * (v + 0.044715 * v**3)))


K, T, S, H, N = 512, 2048, 1024, 512, 128
P = 2 ** 7


def setup_inputs():
    n = np.random.standard_normal
    s = mx_kscale(K)[:, None]
    u = mx_kscale(H)
    packed_w2 = pack_weight(n((H, N)) / np.sqrt(H) / u[:, None])
    return {
        "xT": (n((K, T)) * s).astype(np.float32),
        "gate": np.tile(np.random.uniform(0.2, 1.0, S), (P, 1)).astype(np.float32),
        "res": n((N, T)).astype(np.float32),
        "w1": (n((K, H)) / np.sqrt(K) / s * u).astype(np.float32),
        "w2_words": packed_w2[0],
        "w2_scales": packed_w2[1],
        "offs": striped(np.random.permutation(T)[:S]),
    }


def reference(xT, gate, res, w1, w2_words, w2_scales, offs):
    r = f64(res)[:, unstriped(offs)]
    xq = mxq(f64(xT)[:, unstriped(offs)], 0, "e4m3")
    h = gelu(mxq(f64(w1), 0, "e4m3").T @ xq)
    y = unpack_weight(w2_words, w2_scales).T @ mxq(h, 0, "e4m3")
    out = f64(res).copy()
    out[:, unstriped(offs)] = r + y * f64(gate)[:1]
    return out

@@ -1,0 +1,182 @@
+from contextlib import ExitStack
+
+import concourse.mybir as mybir
+
+K, T, S, H, N = 512, 2048, 1024, 512, 128
+FLOPS = 2 * S * (K * H + H * N)
+
+F32 = mybir.dt.float32
+BF16 = mybir.dt.bfloat16
+I32 = mybir.dt.int32
+U32 = mybir.dt.uint32
+U16 = mybir.dt.uint16
+U8 = mybir.dt.uint8
+FP8X4 = mybir.dt.float8_e4m3fn_x4
+MULT = mybir.AluOpType.mult
+ADD = mybir.AluOpType.add
+GELU = mybir.ActivationFunctionType.Gelu_apprx_tanh
+
+P = 128
+PACK = 4
+CHUNK = 256
+CHUNKS = S // CHUNK
+BLOCK = 128
+LIST_ROWS = 16
+X_PIECES = (
+    ((1024, "vector"), (512, "vector"), (512, "vector")),
+    ((640, "scalar"), (640, "scalar"), (512, "vector"), (256, "vector")),
+)
+W1_PIECES = 2
+
+
+def tile_picked_modres_mlpgelu_l_kernel(tc, xT, gate, res, w1, w2_words, w2_scales, offs, out):
+    nc = tc.nc
+    with ExitStack() as ctx:
+        keep = ctx.enter_context(tc.tile_pool(name="keep", bufs=1))
+        h_psum = ctx.enter_context(tc.psum_pool(name="h_psum", bufs=4))
+        y_psum = ctx.enter_context(tc.psum_pool(name="y_psum", bufs=4))
+
+        offsets = keep.tile([P, S // LIST_ROWS], U16, name="offsets")
+
+        def entries(c):
+            cols = CHUNK // LIST_ROWS
+            return offsets[:, c * cols : (c + 1) * cols]
+
+        warm_in = keep.tile([P, 1], F32, name="warm_in")
+        warm_out = keep.tile([P, 1], F32, name="warm_out")
+        nc.vector.memset(warm_in[:], 0.0)
+        nc.scalar.activation(out=warm_out[:], in_=warm_in[:], func=GELU)
+
+        w2_scale = keep.tile([P, N], U8, name="w2_scale", align_bytes=64)
+        nc.vector.memset(w2_scale[:].bitcast(I32), 0)
+
+        x_rows = xT.rearrange("(p j) t -> p j t", j=PACK)
+        picked = [keep.tile([P, CHUNK, 2], U32, name="picked%d" % c, align_bytes=64) for c in range(CHUNKS)]
+        pairs = []
+        for u, pieces in enumerate(X_PIECES):
+            pair = keep.tile([P, T], U32, name="pair%d" % u, align_bytes=64)
+            pairs.append(pair)
+            col = 0
+            for i, (width, engine) in enumerate(pieces):
+                raw = keep.tile([P, 2, width], F32, name="x_raw%d_%d" % (u, i), align_bytes=64)
+                nc.sync.dma_start(out=raw[:], in_=x_rows[:, 2 * u : 2 * u + 2, col : col + width])
+                if u == 0 and i == 0:
+                    nc.sync.dma_start(offsets[:], offs)
+                dst = pair[:, col : col + width].bitcast(BF16).rearrange("p (c e) -> p c e", e=2)
+                src = raw[:].rearrange("p e c -> p c e")
+                if engine == "vector":
+                    nc.vector.tensor_copy(out=dst, in_=src)
+                else:
+                    nc.scalar.copy(out=dst, in_=src)
+                col = col + width
+            if u == 0:
+                for c in range(CHUNKS):
+                    nc.vector.tensor_copy(out=picked[c][:, :, 0], in_=pair[:].indirect(entries(c)))
+
+        w1_rows = w1.rearrange("(p j) c -> p j c", j=PACK)
+        w1_grouped = keep.tile([P, H * PACK], BF16, name="w1_grouped", tag="late", align_bytes=64)
+        w1_view = w1_grouped[:].rearrange("p (t m j) -> p m t j", t=PACK, j=PACK)
+        cols = H // W1_PIECES
+        for i in range(W1_PIECES):
+            raw = keep.tile([P, PACK, cols], F32, name="w1_raw%d" % i, align_bytes=64)
+            nc.sync.dma_start(out=raw[:], in_=w1_rows[:, :, i * cols : (i + 1) * cols])
+            ms = cols // PACK
+            nc.scalar.copy(
+                out=w1_view[:, i * ms : (i + 1) * ms],
+                in_=raw[:].rearrange("p j (m t) -> p m t j", t=PACK),
+            )
+
+        window = keep.tile([P, T], F32, name="window", align_bytes=64)
+        nc.sync.dma_start(out=window[:], in_=res)
+        w2_codes = keep.tile([P, N], U32, name="w2_codes", align_bytes=64)
+        nc.sync.dma_start(out=w2_codes[:].bitcast(I32), in_=w2_words[0].rearrange("p n r -> p (n r)").bitcast(I32))
+        for q in range(4):
+            nc.sync.dma_start(
+                out=w2_scale[32 * q : 32 * q + 4, :].bitcast(I32),
+                in_=w2_scales[0, 4 * q : 4 * q + 4, :].bitcast(I32),
+            )
+        gates = keep.tile([P, S], F32, name="gates", align_bytes=64)
+        nc.sync.dma_start(out=gates[:], in_=gate)
+
+        for c in range(CHUNKS):
+            nc.vector.tensor_copy(out=picked[c][:, :, 1], in_=pairs[1][:].indirect(entries(c)))
+
+        x_codes, x_scale = [], []
+
+        def quantize_x(c, tag):
+            codes = keep.tile([P, CHUNK], U32, name="x_codes%d" % c, tag=tag, align_bytes=64)
+            scale = keep.tile([P, CHUNK], U8, name="x_scale%d" % c, align_bytes=64)
+            nc.vector.quantize_mx(
+                out=codes[:].bitcast(FP8X4),
+                scales=scale[:],
+                in_=picked[c][:].rearrange("p s u -> p (s u)").bitcast(BF16),
+            )
+            x_codes.append(codes)
+            x_scale.append(scale)
+
+        quantize_x(0, "x_codes0")
+        quantize_x(1, "x_codes1")
+        w1_codes = keep.tile([P, H], U32, name="w1_codes", align_bytes=64)
+        w1_scale = keep.tile([P, H], U8, name="w1_scale", align_bytes=64)
+        nc.vector.quantize_mx(out=w1_codes[:].bitcast(FP8X4), scales=w1_scale[:], in_=w1_grouped[:])
+        quantize_x(2, "late")
+        quantize_x(3, "x_codes3")
+
+        old = []
+        for c in range(CHUNKS):
+            r = keep.tile([P, CHUNK], F32, name="old%d" % c, align_bytes=64)
+            nc.vector.tensor_copy(out=r[:], in_=window[:].indirect(entries(c)))
+            old.append(r)
+
+        def first_product(c):
+            hidden = keep.tile([P, CHUNK, PACK], BF16, name="hidden%d" % c, tag="hidden%d" % c, align_bytes=64)
+            for b in range(CHUNK // BLOCK):
+                toks = slice(b * BLOCK, (b + 1) * BLOCK)
+                acc = h_psum.tile([P, PACK, BLOCK], F32, name="acc")
+                for t in range(PACK):
+                    chans = slice(t * P, (t + 1) * P)
+                    nc.tensor.matmul_mx(
+                        out=acc[:, t, :],
+                        lhsT=w1_codes[:, chans].bitcast(FP8X4),
+                        lhsT_scale=w1_scale[:, chans],
+                        rhs=x_codes[c][:, toks].bitcast(FP8X4),
+                        rhs_scale=x_scale[c][:, toks],
+                        start=True,
+                        stop=True,
+                    )
+                nc.scalar.activation(out=hidden[:, toks, :], in_=acc[:].rearrange("p t s -> p s t"), func=GELU)
+            return hidden
+
+        def second_product(c, hidden):
+            codes = keep.tile([P, CHUNK], U32, name="h_codes%d" % c, align_bytes=64)
+            scale = keep.tile([P, CHUNK], U8, name="h_scale%d" % c, align_bytes=64)
+            nc.vector.quantize_mx(
+                out=codes[:].bitcast(FP8X4), scales=scale[:], in_=hidden[:].rearrange("p s t -> p (s t)")
+            )
+            y = y_psum.tile([P, CHUNK], F32, name="y")
+            nc.tensor.matmul_mx(
+                out=y[:],
+                lhsT=w2_codes[:].bitcast(FP8X4),
+                lhsT_scale=w2_scale[:],
+                rhs=codes[:].bitcast(FP8X4),
+                rhs_scale=scale[:],
+                start=True,
+                stop=True,
+            )
+            return y
+
+        def put_back(c, y):
+            tag = "hidden%d" % (c + 1) if c + 1 < CHUNKS else "weighted_last"
+            weighted = keep.tile([P, CHUNK], F32, name="weighted%d" % c, tag=tag, align_bytes=64)
+            nc.vector.tensor_tensor(out=weighted[:], in0=y[:], in1=gates[:, c * CHUNK : (c + 1) * CHUNK], op=MULT)
+            nc.vector.tensor_tensor(out=window[:].indirect(entries(c)), in0=weighted[:], in1=old[c][:], op=ADD)
+
+        hiddens = [first_product(c) for c in range(CHUNKS)]
+        ys = []
+        for c in range(CHUNKS):
+            ys.append(second_product(c, hiddens[c]))
+            if c >= 1:
+                put_back(c - 1, ys[c - 1])
+        put_back(CHUNKS - 1, ys[CHUNKS - 1])
+
+        nc.sync.dma_start(out=out, in_=window[:])

@@ -23,9 +23,10 @@ CHUNKS = S // CHUNK
 BLOCK = 128
 LIST_ROWS = 16
 X_PIECES = (
-    ((1024, "vector"), (512, "vector"), (512, "vector")),
-    ((640, "scalar"), (640, "scalar"), (512, "vector"), (256, "vector")),
+    ((1024, 1024), (1024, 640)),
+    ((768, 0), (768, 384), (512, 320)),
 )
+WOVEN_FROM = 2
 W1_PIECES = 2
 
 
@@ -51,34 +52,40 @@ def tile_picked_modres_mlpgelu_l_kernel(tc, xT, gate, res, w1, w2_words, w2_scal
         nc.vector.memset(w2_scale[:].bitcast(I32), 0)
 
         x_rows = xT.rearrange("(p j) t -> p j t", j=PACK)
-        picked = [keep.tile([P, CHUNK, 2], U32, name="picked%d" % c, align_bytes=64) for c in range(CHUNKS)]
+        picked = [keep.tile([P, CHUNK, 2], U32, name="picked%d" % c, align_bytes=64)[:] for c in range(WOVEN_FROM)]
+        halves = {c: keep.tile([P, 2, CHUNK], U32, name="halves%d" % c, align_bytes=64) for c in range(WOVEN_FROM, CHUNKS)}
+
+        def fetch_pair(u, c, pair):
+            dst = picked[c][:, :, u] if c < WOVEN_FROM else halves[c][:, u, :]
+            nc.vector.tensor_copy(out=dst, in_=pair[:].indirect(entries(c)))
+
         pairs = []
         for u, pieces in enumerate(X_PIECES):
             pair = keep.tile([P, T], U32, name="pair%d" % u, align_bytes=64)
             pairs.append(pair)
             col = 0
-            for i, (width, engine) in enumerate(pieces):
+            for i, (width, on_vector) in enumerate(pieces):
                 raw = keep.tile([P, 2, width], F32, name="x_raw%d_%d" % (u, i), align_bytes=64)
                 nc.sync.dma_start(out=raw[:], in_=x_rows[:, 2 * u : 2 * u + 2, col : col + width])
                 if u == 0 and i == 0:
                     nc.sync.dma_start(offsets[:], offs)
                 dst = pair[:, col : col + width].bitcast(BF16).rearrange("p (c e) -> p c e", e=2)
                 src = raw[:].rearrange("p e c -> p c e")
-                if engine == "vector":
-                    nc.vector.tensor_copy(out=dst, in_=src)
-                else:
-                    nc.scalar.copy(out=dst, in_=src)
+                if on_vector > 0:
+                    nc.vector.tensor_copy(out=dst[:, :on_vector], in_=src[:, :on_vector])
+                if on_vector < width:
+                    nc.scalar.copy(out=dst[:, on_vector:], in_=src[:, on_vector:])
                 col = col + width
             if u == 0:
                 for c in range(CHUNKS):
-                    nc.vector.tensor_copy(out=picked[c][:, :, 0], in_=pair[:].indirect(entries(c)))
+                    fetch_pair(0, c, pair)
 
         w1_rows = w1.rearrange("(p j) c -> p j c", j=PACK)
-        w1_grouped = keep.tile([P, H * PACK], BF16, name="w1_grouped", tag="late", align_bytes=64)
+        w1_grouped = keep.tile([P, H * PACK], BF16, name="w1_grouped", align_bytes=64)
         w1_view = w1_grouped[:].rearrange("p (t m j) -> p m t j", t=PACK, j=PACK)
         cols = H // W1_PIECES
         for i in range(W1_PIECES):
-            raw = keep.tile([P, PACK, cols], F32, name="w1_raw%d" % i, align_bytes=64)
+            raw = keep.tile([P, PACK, cols], F32, name="w1_raw%d" % i, tag="w1_raw%d" % i, align_bytes=64)
             nc.sync.dma_start(out=raw[:], in_=w1_rows[:, :, i * cols : (i + 1) * cols])
             ms = cols // PACK
             nc.scalar.copy(
@@ -98,8 +105,12 @@ def tile_picked_modres_mlpgelu_l_kernel(tc, xT, gate, res, w1, w2_words, w2_scal
         gates = keep.tile([P, S], F32, name="gates", align_bytes=64)
         nc.sync.dma_start(out=gates[:], in_=gate)
 
+        woven = keep.tile([P, (CHUNKS - WOVEN_FROM) * CHUNK, 2], U32, name="woven", tag="w1_raw1", align_bytes=64)
         for c in range(CHUNKS):
-            nc.vector.tensor_copy(out=picked[c][:, :, 1], in_=pairs[1][:].indirect(entries(c)))
+            fetch_pair(1, c, pairs[1])
+            if c >= WOVEN_FROM:
+                picked.append(woven[:, (c - WOVEN_FROM) * CHUNK : (c - WOVEN_FROM + 1) * CHUNK, :])
+                nc.scalar.copy(out=picked[c], in_=halves[c][:].rearrange("p u s -> p s u"))
 
         x_codes, x_scale = [], []
 
@@ -109,7 +120,7 @@ def tile_picked_modres_mlpgelu_l_kernel(tc, xT, gate, res, w1, w2_words, w2_scal
             nc.vector.quantize_mx(
                 out=codes[:].bitcast(FP8X4),
                 scales=scale[:],
-                in_=picked[c][:].rearrange("p s u -> p (s u)").bitcast(BF16),
+                in_=picked[c].rearrange("p s u -> p (s u)").bitcast(BF16),
             )
             x_codes.append(codes)
             x_scale.append(scale)
@@ -119,7 +130,7 @@ def tile_picked_modres_mlpgelu_l_kernel(tc, xT, gate, res, w1, w2_words, w2_scal
         w1_codes = keep.tile([P, H], U32, name="w1_codes", align_bytes=64)
         w1_scale = keep.tile([P, H], U8, name="w1_scale", align_bytes=64)
         nc.vector.quantize_mx(out=w1_codes[:].bitcast(FP8X4), scales=w1_scale[:], in_=w1_grouped[:])
-        quantize_x(2, "late")
+        quantize_x(2, "x_codes2")
         quantize_x(3, "x_codes3")
 
         old = []

from contextlib import ExitStack

import concourse.mybir as mybir

K, T, S, H, N = 512, 2048, 1024, 512, 128
FLOPS = 2 * S * (K * H + H * N)

F32 = mybir.dt.float32
BF16 = mybir.dt.bfloat16
I32 = mybir.dt.int32
U32 = mybir.dt.uint32
U16 = mybir.dt.uint16
U8 = mybir.dt.uint8
FP8X4 = mybir.dt.float8_e4m3fn_x4
MULT = mybir.AluOpType.mult
ADD = mybir.AluOpType.add
GELU = mybir.ActivationFunctionType.Gelu_apprx_tanh

P = 128
PACK = 4
CHUNK = 256
CHUNKS = S // CHUNK
BLOCK = 128
LIST_ROWS = 16
X_PIECES = (
    ((1024, 1024), (1024, 640)),
    ((768, 0), (768, 384), (512, 320)),
)
WOVEN_FROM = 2
W1_PIECES = 2


def tile_picked_modres_mlpgelu_l_kernel(tc, xT, gate, res, w1, w2_words, w2_scales, offs, out):
    nc = tc.nc
    with ExitStack() as ctx:
        keep = ctx.enter_context(tc.tile_pool(name="keep", bufs=1))
        h_psum = ctx.enter_context(tc.psum_pool(name="h_psum", bufs=4))
        y_psum = ctx.enter_context(tc.psum_pool(name="y_psum", bufs=4))

        offsets = keep.tile([P, S // LIST_ROWS], U16, name="offsets")

        def entries(c):
            cols = CHUNK // LIST_ROWS
            return offsets[:, c * cols : (c + 1) * cols]

        warm_in = keep.tile([P, 1], F32, name="warm_in")
        warm_out = keep.tile([P, 1], F32, name="warm_out")
        nc.vector.memset(warm_in[:], 0.0)
        nc.scalar.activation(out=warm_out[:], in_=warm_in[:], func=GELU)

        w2_scale = keep.tile([P, N], U8, name="w2_scale", align_bytes=64)
        nc.vector.memset(w2_scale[:].bitcast(I32), 0)

        x_rows = xT.rearrange("(p j) t -> p j t", j=PACK)
        picked = [keep.tile([P, CHUNK, 2], U32, name="picked%d" % c, align_bytes=64)[:] for c in range(WOVEN_FROM)]
        halves = {c: keep.tile([P, 2, CHUNK], U32, name="halves%d" % c, align_bytes=64) for c in range(WOVEN_FROM, CHUNKS)}

        def fetch_pair(u, c, pair):
            dst = picked[c][:, :, u] if c < WOVEN_FROM else halves[c][:, u, :]
            nc.vector.tensor_copy(out=dst, in_=pair[:].indirect(entries(c)))

        pairs = []
        for u, pieces in enumerate(X_PIECES):
            pair = keep.tile([P, T], U32, name="pair%d" % u, align_bytes=64)
            pairs.append(pair)
            col = 0
            for i, (width, on_vector) in enumerate(pieces):
                raw = keep.tile([P, 2, width], F32, name="x_raw%d_%d" % (u, i), align_bytes=64)
                nc.sync.dma_start(out=raw[:], in_=x_rows[:, 2 * u : 2 * u + 2, col : col + width])
                if u == 0 and i == 0:
                    nc.sync.dma_start(offsets[:], offs)
                dst = pair[:, col : col + width].bitcast(BF16).rearrange("p (c e) -> p c e", e=2)
                src = raw[:].rearrange("p e c -> p c e")
                if on_vector > 0:
                    nc.vector.tensor_copy(out=dst[:, :on_vector], in_=src[:, :on_vector])
                if on_vector < width:
                    nc.scalar.copy(out=dst[:, on_vector:], in_=src[:, on_vector:])
                col = col + width
            if u == 0:
                for c in range(CHUNKS):
                    fetch_pair(0, c, pair)

        w1_rows = w1.rearrange("(p j) c -> p j c", j=PACK)
        w1_grouped = keep.tile([P, H * PACK], BF16, name="w1_grouped", align_bytes=64)
        w1_view = w1_grouped[:].rearrange("p (t m j) -> p m t j", t=PACK, j=PACK)
        cols = H // W1_PIECES
        for i in range(W1_PIECES):
            raw = keep.tile([P, PACK, cols], F32, name="w1_raw%d" % i, tag="w1_raw%d" % i, align_bytes=64)
            nc.sync.dma_start(out=raw[:], in_=w1_rows[:, :, i * cols : (i + 1) * cols])
            ms = cols // PACK
            nc.scalar.copy(
                out=w1_view[:, i * ms : (i + 1) * ms],
                in_=raw[:].rearrange("p j (m t) -> p m t j", t=PACK),
            )

        window = keep.tile([P, T], F32, name="window", align_bytes=64)
        nc.sync.dma_start(out=window[:], in_=res)
        w2_codes = keep.tile([P, N], U32, name="w2_codes", align_bytes=64)
        nc.sync.dma_start(out=w2_codes[:].bitcast(I32), in_=w2_words[0].rearrange("p n r -> p (n r)").bitcast(I32))
        for q in range(4):
            nc.sync.dma_start(
                out=w2_scale[32 * q : 32 * q + 4, :].bitcast(I32),
                in_=w2_scales[0, 4 * q : 4 * q + 4, :].bitcast(I32),
            )
        gates = keep.tile([P, S], F32, name="gates", align_bytes=64)
        nc.sync.dma_start(out=gates[:], in_=gate)

        woven = keep.tile([P, (CHUNKS - WOVEN_FROM) * CHUNK, 2], U32, name="woven", tag="w1_raw1", align_bytes=64)
        for c in range(CHUNKS):
            fetch_pair(1, c, pairs[1])
            if c >= WOVEN_FROM:
                picked.append(woven[:, (c - WOVEN_FROM) * CHUNK : (c - WOVEN_FROM + 1) * CHUNK, :])
                nc.scalar.copy(out=picked[c], in_=halves[c][:].rearrange("p u s -> p s u"))

        x_codes, x_scale = [], []

        def quantize_x(c, tag):
            codes = keep.tile([P, CHUNK], U32, name="x_codes%d" % c, tag=tag, align_bytes=64)
            scale = keep.tile([P, CHUNK], U8, name="x_scale%d" % c, align_bytes=64)
            nc.vector.quantize_mx(
                out=codes[:].bitcast(FP8X4),
                scales=scale[:],
                in_=picked[c].rearrange("p s u -> p (s u)").bitcast(BF16),
            )
            x_codes.append(codes)
            x_scale.append(scale)

        quantize_x(0, "x_codes0")
        quantize_x(1, "x_codes1")
        w1_codes = keep.tile([P, H], U32, name="w1_codes", align_bytes=64)
        w1_scale = keep.tile([P, H], U8, name="w1_scale", align_bytes=64)
        nc.vector.quantize_mx(out=w1_codes[:].bitcast(FP8X4), scales=w1_scale[:], in_=w1_grouped[:])
        quantize_x(2, "x_codes2")
        quantize_x(3, "x_codes3")

        old = []
        for c in range(CHUNKS):
            r = keep.tile([P, CHUNK], F32, name="old%d" % c, align_bytes=64)
            nc.vector.tensor_copy(out=r[:], in_=window[:].indirect(entries(c)))
            old.append(r)

        def first_product(c):
            hidden = keep.tile([P, CHUNK, PACK], BF16, name="hidden%d" % c, tag="hidden%d" % c, align_bytes=64)
            for b in range(CHUNK // BLOCK):
                toks = slice(b * BLOCK, (b + 1) * BLOCK)
                acc = h_psum.tile([P, PACK, BLOCK], F32, name="acc")
                for t in range(PACK):
                    chans = slice(t * P, (t + 1) * P)
                    nc.tensor.matmul_mx(
                        out=acc[:, t, :],
                        lhsT=w1_codes[:, chans].bitcast(FP8X4),
                        lhsT_scale=w1_scale[:, chans],
                        rhs=x_codes[c][:, toks].bitcast(FP8X4),
                        rhs_scale=x_scale[c][:, toks],
                        start=True,
                        stop=True,
                    )
                nc.scalar.activation(out=hidden[:, toks, :], in_=acc[:].rearrange("p t s -> p s t"), func=GELU)
            return hidden

        def second_product(c, hidden):
            codes = keep.tile([P, CHUNK], U32, name="h_codes%d" % c, align_bytes=64)
            scale = keep.tile([P, CHUNK], U8, name="h_scale%d" % c, align_bytes=64)
            nc.vector.quantize_mx(
                out=codes[:].bitcast(FP8X4), scales=scale[:], in_=hidden[:].rearrange("p s t -> p (s t)")
            )
            y = y_psum.tile([P, CHUNK], F32, name="y")
            nc.tensor.matmul_mx(
                out=y[:],
                lhsT=w2_codes[:].bitcast(FP8X4),
                lhsT_scale=w2_scale[:],
                rhs=codes[:].bitcast(FP8X4),
                rhs_scale=scale[:],
                start=True,
                stop=True,
            )
            return y

        def put_back(c, y):
            tag = "hidden%d" % (c + 1) if c + 1 < CHUNKS else "weighted_last"
            weighted = keep.tile([P, CHUNK], F32, name="weighted%d" % c, tag=tag, align_bytes=64)
            nc.vector.tensor_tensor(out=weighted[:], in0=y[:], in1=gates[:, c * CHUNK : (c + 1) * CHUNK], op=MULT)
            nc.vector.tensor_tensor(out=window[:].indirect(entries(c)), in0=weighted[:], in1=old[c][:], op=ADD)

        hiddens = [first_product(c) for c in range(CHUNKS)]
        ys = []
        for c in range(CHUNKS):
            ys.append(second_product(c, hiddens[c]))
            if c >= 1:
                put_back(c - 1, ys[c - 1])
        put_back(CHUNKS - 1, ys[CHUNKS - 1])

        nc.sync.dma_start(out=out, in_=window[:])
